import numpy as np
import ml_dtypes


def mxq(x, axis, fmt="e4m3"):
    dtype, down = {"e4m3": (ml_dtypes.float8_e4m3fn, 7), "e5m2": (ml_dtypes.float8_e5m2, 14)}[fmt]
    v = np.moveaxis(np.asarray(x, np.float32).astype(ml_dtypes.bfloat16).astype(np.float64), axis, -1)
    blocks = v.reshape(v.shape[:-1] + (-1, 32))
    amax = np.abs(blocks).max(-1, keepdims=True)
    byte = np.maximum(np.where(amax > 0, np.frexp(amax)[1] - 1 + 127, 0) - down, 1)
    scale = np.exp2(byte - 127.0)
    codes = (blocks / scale).astype(np.float32).astype(dtype).astype(np.float64)
    return np.moveaxis((codes * scale).reshape(v.shape), -1, axis)


WIDE = False


def mx_kscale(k):
    if not WIDE:
        return np.ones(k)
    levels = np.array([10, -10, 5, -5, 0])
    if k % 512:
        return np.exp2(np.random.permutation(np.resize(levels, k // 32))).repeat(32)
    a = np.empty((k // 512, 16))
    for p in range(k // 512):
        a[p, :8] = np.random.permutation(np.resize(levels, 8))
        for g in range(8):
            far = levels[np.abs(levels - a[p, g]) >= 10]
            a[p, g + 8] = far[np.random.randint(len(far))]
    return np.exp2(a.ravel()).repeat(32)


def f64(x):
    return np.asarray(x).astype(np.float64)


def striped(idx):
    return np.tile(idx.reshape(-1, 16).T, (8, 1)).astype(np.uint16)


def unstriped(offs):
    return offs[:16].T.reshape(-1).astype(np.int64)


def pack_weight(w):
    k, n = w.shape
    w = f64(np.asarray(w, np.float32).astype(ml_dtypes.bfloat16)).reshape(k // 32, 32, n)
    amax = np.abs(w).max(1)
    byte = np.clip(np.where(amax > 0, np.frexp(amax)[1] - 1 + 127 - 7, 1), 1, 254)
    scaled = (w * np.exp2(127.0 - byte)[:, None, :]).reshape(k, n).astype(np.float32)
    words = np.ascontiguousarray(scaled.reshape(k // 512, 128, 4, n).transpose(0, 1, 3, 2)).astype(ml_dtypes.float8_e4m3fn).view(np.uint8)
    return words, np.ascontiguousarray(byte.astype(np.uint8).reshape(k // 512, 16, n))


def unpack_weight(words, scales):
    g, p, n, _ = words.shape
    vals = np.ascontiguousarray(words).view(ml_dtypes.float8_e4m3fn).astype(np.float64) * np.repeat(np.exp2(scales.astype(np.float64) - 127.0), 8, axis=1)[..., None]
    return vals.transpose(0, 1, 3, 2).reshape(g * 512, n)


def relu(v):
    return np.maximum(v, 0.0)


K, T, S, V, R, W = 512, 2048, 512, 512, 256, 1024
P = 2 ** 7


def setup_inputs():
    n = np.random.standard_normal
    s = mx_kscale(K)[:, None]
    packed_xT = pack_weight(n((K, T)) * s)
    packed_eT = pack_weight(n((K, W)) * s)
    return {
        "x_words": packed_xT[0],
        "x_scales": packed_xT[1],
        "hT": (n((K, V)) / np.sqrt(K) / s).astype(np.float32),
        "e_words": packed_eT[0],
        "e_scales": packed_eT[1],
        "totl": (np.tile(np.random.uniform(150.0, 300.0, W), (P, 1))).astype(np.float32),
        "bow": (np.tile(np.random.uniform(0.2, 0.7, T), (P, 1))).astype(np.float32),
        "tot": (np.tile(np.random.uniform(20.0, 60.0, T), (P, 1))).astype(np.float32),
        "offs": striped(np.random.permutation(T)[:S]),
        "low": striped(np.random.permutation(W)[:R]),
        "suf": striped(np.random.permutation(np.concatenate([np.arange(R), np.random.randint(0, R, S - R)]))),
    }


def reference(x_words, x_scales, hT, e_words, e_scales, totl, bow, tot, offs, low, suf):
    hTq = mxq(f64(hT), 0, "e4m3")
    xq = unpack_weight(x_words, x_scales)[:, unstriped(offs)]
    y = hTq.T @ xq
    ca = np.exp(0.8 * y)
    da = relu(ca - 0.75)
    e_low = unpack_weight(e_words, e_scales)[:, unstriped(low)]
    z = hTq.T @ e_low
    cl = np.exp(0.8 * z)
    tl = f64(totl)[:1][:, unstriped(low)]
    plow = cl / tl
    return 100.0 * (da / (f64(tot)[:1][:, unstriped(offs)]) + (f64(bow)[:1][:, unstriped(offs)]) * plow[:, unstriped(suf)])

@@ -1,0 +1,222 @@
+from contextlib import ExitStack
+
+import concourse.mybir as mybir
+from concourse.masks import make_identity
+
+K, T, S, V, R, W = 512, 2048, 512, 512, 256, 1024
+P = 128
+PACK = 4
+FLOPS = 2 * K * V * (S + R)
+BYTES = K * (T + W) + (K // 32) * (T + W) + 4 * K * V + 4 * (2 * T + W) + 2 * P * (2 * S + R) // 16 + 4 * V * S
+
+F32 = mybir.dt.float32
+BF16 = mybir.dt.bfloat16
+I32 = mybir.dt.int32
+U32 = mybir.dt.uint32
+U16 = mybir.dt.uint16
+U8 = mybir.dt.uint8
+FP8X4 = mybir.dt.float8_e4m3fn_x4
+ALU = mybir.AluOpType
+ACT = mybir.ActivationFunctionType
+
+TOT_ROW, BOW_ROW, TOTL_ROW = 4, 8, 12
+HALF = 256
+SPARE = 16
+
+
+def tile_picked_ybackof_prob_p_kernel(
+    tc, x_words, x_scales, hT, e_words, e_scales, totl, bow, tot, offs, low, suf, out
+):
+    nc = tc.nc
+    with ExitStack() as ctx:
+        keep = ctx.enter_context(tc.tile_pool(name="keep", bufs=1))
+        psum = ctx.enter_context(tc.psum_pool(name="psum", bufs=1))
+
+        low_sb = keep.tile([P, R // 16], U16, name="low_sb")
+        offs_sb = keep.tile([P, S // 16], U16, name="offs_sb")
+        suf_sb = keep.tile([P, S // 16], U16, name="suf_sb")
+        e_scale_tab = keep.tile([P, W], U8, name="e_scale_tab", align_bytes=64)
+        x_scale_tab = keep.tile([P, T], U8, name="x_scale_tab", align_bytes=64)
+        rows = keep.tile([P, T], F32, name="rows", align_bytes=64)
+        nc.vector.memset(e_scale_tab[:].bitcast(I32), 0)
+        nc.vector.memset(rows[:], 0.0)
+        nc.vector.memset(x_scale_tab[:].bitcast(I32), 0)
+
+        ident = keep.tile([P, P], F32, name="ident", align_bytes=64)
+        make_identity(nc, ident[:])
+        warm = keep.tile([P, 1], F32, name="warm")
+        nc.scalar.activation(warm[:], ident[:, 0:1], ACT.Exp)
+
+        def load_scale_rows(table, scales):
+            for q in range(4):
+                nc.sync.dma_start(
+                    table[32 * q : 32 * q + 4, :].bitcast(I32), scales[0, 4 * q : 4 * q + 4, :].bitcast(I32)
+                )
+
+        def load_words(table, words):
+            nc.sync.dma_start(table[:].bitcast(I32), words[0].rearrange("p n t -> p (n t)").bitcast(I32))
+
+        e_word_tab = keep.tile([P, W], U32, name="e_word_tab", align_bytes=64)
+        x_word_tab = keep.tile([P, T], U32, name="x_word_tab", tag="x_words_then_backoff", align_bytes=64)
+        h_raw = [keep.tile([P, PACK, HALF], F32, name=f"h_raw{c}", align_bytes=64) for c in range(2)]
+        h_rows = hT.rearrange("(p j) t -> p j t", j=PACK)
+
+        nc.sync.dma_start(low_sb[:], low)
+        load_words(e_word_tab, e_words)
+        load_scale_rows(e_scale_tab, e_scales)
+        nc.sync.dma_start(offs_sb[:], offs)
+        nc.sync.dma_start(h_raw[0][:], h_rows[:, :, 0:HALF])
+        nc.sync.dma_start(rows[TOTL_ROW : TOTL_ROW + 1, 0:W], totl[0:1, :])
+        nc.sync.dma_start(rows[TOT_ROW : TOT_ROW + 1, :], tot[0:1, :])
+        nc.sync.dma_start(rows[BOW_ROW : BOW_ROW + 1, :], bow[0:1, :])
+        load_words(x_word_tab, x_words)
+        load_scale_rows(x_scale_tab, x_scales)
+        nc.sync.dma_start(h_raw[1][:], h_rows[:, :, HALF:])
+        nc.sync.dma_start(suf_sb[:], suf)
+
+        plow = []
+        for t in range(4):
+            window = keep.tile([P, R + SPARE], F32, name=f"plow{t}", align_bytes=64)
+            nc.gpsimd.memset(window[:, R:], 0.0)
+            plow.append(window)
+
+        e_codes = keep.tile([P, R], U32, name="e_codes", align_bytes=64)
+        e_plane = keep.tile([P, R], U8, name="e_plane", align_bytes=64)
+        nc.vector.tensor_copy(e_codes[:], e_word_tab[:].indirect(low_sb[:]))
+        nc.vector.tensor_copy(e_plane[:], e_scale_tab[:].indirect(low_sb[:]))
+
+        by_low = keep.tile([P, R], F32, name="by_low", align_bytes=64)
+        by_offs = keep.tile([P, S], F32, name="by_offs", align_bytes=64)
+        nc.vector.tensor_copy(by_low[:], rows[:].indirect(low_sb[:]))
+        nc.vector.tensor_copy(by_offs[:], rows[:].indirect(offs_sb[:]))
+
+        low_turned = psum.tile([P, 2, P], F32, name="low_turned", tag="bank_y1")
+        for c in range(2):
+            nc.tensor.transpose(low_turned[:, c, :], by_low[:, c * P : (c + 1) * P], ident[:])
+        inv_totl = keep.tile([P, 2], F32, name="inv_totl")
+        nc.vector.reciprocal(inv_totl[:], low_turned[:, :, TOTL_ROW])
+        inv_totl_row = psum.tile([P, R], F32, name="inv_totl_row", tag="bank_r")
+        for c in range(2):
+            nc.tensor.transpose(
+                inv_totl_row[:, c * P : (c + 1) * P], inv_totl[:, c : c + 1].to_broadcast([P, P]), ident[:]
+            )
+
+        offs_turned = psum.tile([P, 4, P], F32, name="offs_turned", tag="bank_y0")
+        for c in range(4):
+            nc.tensor.transpose(offs_turned[:, c, :], by_offs[:, c * P : (c + 1) * P], ident[:])
+        inv_tot = keep.tile([P, 4], F32, name="inv_tot")
+        nc.vector.reciprocal(inv_tot[:], offs_turned[:, :, TOT_ROW])
+        bow100 = keep.tile([P, 4], F32, name="bow100")
+        nc.scalar.mul(bow100[:], offs_turned[:, :, BOW_ROW], 100.0)
+        gain = keep.tile([P, 4], F32, name="gain")
+        nc.scalar.mul(gain[:], inv_tot[:], 100.0)
+        shift = keep.tile([P, 4], F32, name="shift")
+        nc.scalar.mul(shift[:], inv_tot[:], -75.0)
+        bow_bank = psum.tile([P, S], F32, name="bow_bank", tag="bank_y1")
+        for c in range(4):
+            nc.tensor.transpose(
+                bow_bank[:, c * P : (c + 1) * P], bow100[:, c : c + 1].to_broadcast([P, P]), ident[:]
+            )
+        bow_row = keep.tile([P, S], F32, name="bow_row", align_bytes=64)
+        nc.scalar.copy(bow_row[:], bow_bank[:])
+
+        h_codes = keep.tile([P, V], U32, name="h_codes", align_bytes=64)
+        h_plane = keep.tile([P, V], U8, name="h_plane", align_bytes=64)
+        for t in range(4):
+            cols = slice(t * P, (t + 1) * P)
+            grouped = keep.tile([P, P, PACK], BF16, name=f"grouped{t}", align_bytes=64)
+            src = h_raw[t // 2][:, :, (t % 2) * P : (t % 2 + 1) * P]
+            nc.scalar.copy(
+                grouped[:].rearrange("p (c i) j -> p c j i", i=4),
+                src.rearrange("p j (c i) -> p c j i", i=4),
+            )
+            nc.vector.quantize_mx(
+                out=h_codes[:, cols].bitcast(FP8X4),
+                scales=h_plane[:, cols],
+                in_=grouped[:].rearrange("p c j -> p (c j)"),
+            )
+        for t in range(4):
+            cols = slice(t * P, (t + 1) * P)
+            z_bank = psum.tile([P, R], F32, name=f"z_bank{t}", tag="bank_z")
+            nc.tensor.matmul_mx(
+                out=z_bank[:],
+                lhsT=h_codes[:, cols].bitcast(FP8X4),
+                lhsT_scale=h_plane[:, cols],
+                rhs=e_codes[:].bitcast(FP8X4),
+                rhs_scale=e_plane[:],
+                start=True,
+                stop=True,
+            )
+            counts_low = keep.tile([P, R], F32, name=f"counts_low{t}", align_bytes=64)
+            nc.scalar.activation(counts_low[:], z_bank[:], ACT.Exp, scale=0.8)
+            nc.vector.tensor_tensor(plow[t][:, 0:R], counts_low[:], inv_totl_row[:], ALU.mult)
+
+        out_banks = [psum.tile([P, S], F32, name=f"out_bank{t}", tag=f"bank_o{t}") for t in range(4)]
+        for t in range(4):
+            for c in range(4):
+                nc.tensor.matmul(
+                    out_banks[t][:, c * P : (c + 1) * P],
+                    shift[:, c : c + 1].to_broadcast([P, P]),
+                    ident[:],
+                    start=(c == 0),
+                    stop=False,
+                    is_transpose=True,
+                )
+
+        x_codes = keep.tile([P, S], U32, name="x_codes", align_bytes=64)
+        x_plane = keep.tile([P, S], U8, name="x_plane", align_bytes=64)
+        for h in range(2):
+            cols = slice(h * HALF, (h + 1) * HALF)
+            piece = offs_sb[:, h * 16 : (h + 1) * 16]
+            nc.vector.tensor_copy(x_codes[:, cols], x_word_tab[:].indirect(piece))
+            nc.vector.tensor_copy(x_plane[:, cols], x_scale_tab[:].indirect(piece))
+
+        def gather_backoff(t, term):
+            for h in range(2):
+                cols = slice(h * HALF, (h + 1) * HALF)
+                nc.vector.tensor_tensor(
+                    term[:, cols],
+                    plow[t][:].indirect(suf_sb[:, h * 16 : (h + 1) * 16]),
+                    bow_row[:, cols],
+                    ALU.mult,
+                )
+
+        early = keep.tile([P, 2 * S], F32, name="backoff01", tag="x_words_then_backoff", align_bytes=64)
+        backoff = [early[:, 0:S], early[:, S:]]
+        for c in range(4):
+            cols = slice(c * P, (c + 1) * P)
+            y_bank = psum.tile([P, V], F32, name=f"y_bank{c}", tag=f"bank_y{c % 2}")
+            nc.tensor.matmul_mx(
+                out=y_bank[:],
+                lhsT=x_codes[:, cols].bitcast(FP8X4),
+                lhsT_scale=x_plane[:, cols],
+                rhs=h_codes[:].bitcast(FP8X4),
+                rhs_scale=h_plane[:],
+                start=True,
+                stop=True,
+            )
+            counts = keep.tile([P, V], F32, name=f"counts{c}", tag=f"counts{c}", align_bytes=64)
+            nc.scalar.activation(counts[:], y_bank[:], ACT.Exp, scale=0.8)
+            if c % 2 == 0:
+                gather_backoff(c // 2, backoff[c // 2])
+            scaled = keep.tile([P, V], F32, name=f"scaled{c}", align_bytes=64)
+            nc.vector.tensor_scalar(scaled[:], counts[:], 0.75, gain[:, c : c + 1], ALU.max, ALU.mult)
+            for t in range(4):
+                nc.tensor.matmul(
+                    out_banks[t][:, cols],
+                    scaled[:, t * P : (t + 1) * P],
+                    ident[:],
+                    start=False,
+                    stop=(c == 3),
+                    is_transpose=True,
+                )
+            if c % 2 == 1:
+                late = keep.tile([P, S], F32, name=f"backoff{2 + c // 2}", tag=f"counts{c}", align_bytes=64)
+                backoff.append(late[:])
+        for t in (2, 3):
+            gather_backoff(t, backoff[t])
+
+        for t in range(4):
+            result = keep.tile([P, S], F32, name=f"result{t}", align_bytes=64)
+            nc.vector.tensor_tensor(result[:], out_banks[t][:], backoff[t], ALU.add)
+            nc.sync.dma_start(out[t * P : (t + 1) * P, :], result[:])

@@ -22,6 +22,7 @@ ACT = mybir.ActivationFunctionType
 TOT_ROW, BOW_ROW, TOTL_ROW = 4, 8, 12
 HALF = 256
 SPARE = 16
+WIDE = 704
 
 
 def tile_picked_ybackof_prob_p_kernel(
@@ -57,28 +58,28 @@ def tile_picked_ybackof_prob_p_kernel(
             nc.sync.dma_start(table[:].bitcast(I32), words[0].rearrange("p n t -> p (n t)").bitcast(I32))
 
         e_word_tab = keep.tile([P, W], U32, name="e_word_tab", align_bytes=64)
-        x_word_tab = keep.tile([P, T], U32, name="x_word_tab", tag="x_words_then_backoff", align_bytes=64)
-        h_raw = [keep.tile([P, PACK, HALF], F32, name=f"h_raw{c}", align_bytes=64) for c in range(2)]
+        x_word_tab = keep.tile([P, T], U32, name="x_word_tab", align_bytes=64)
+        h_raw = [keep.tile([P, PACK, HALF], F32, name=f"h_raw{c}", tag=f"h_raw{c}", align_bytes=64) for c in range(2)]
         h_rows = hT.rearrange("(p j) t -> p j t", j=PACK)
 
-        nc.sync.dma_start(low_sb[:], low)
         load_words(e_word_tab, e_words)
+        nc.sync.dma_start(low_sb[:], low)
         load_scale_rows(e_scale_tab, e_scales)
         nc.sync.dma_start(offs_sb[:], offs)
         nc.sync.dma_start(h_raw[0][:], h_rows[:, :, 0:HALF])
-        nc.sync.dma_start(rows[TOTL_ROW : TOTL_ROW + 1, 0:W], totl[0:1, :])
         nc.sync.dma_start(rows[TOT_ROW : TOT_ROW + 1, :], tot[0:1, :])
         nc.sync.dma_start(rows[BOW_ROW : BOW_ROW + 1, :], bow[0:1, :])
+        nc.sync.dma_start(rows[TOTL_ROW : TOTL_ROW + 1, 0:W], totl[0:1, :])
         load_words(x_word_tab, x_words)
         load_scale_rows(x_scale_tab, x_scales)
         nc.sync.dma_start(h_raw[1][:], h_rows[:, :, HALF:])
         nc.sync.dma_start(suf_sb[:], suf)
 
-        plow = []
-        for t in range(4):
-            window = keep.tile([P, R + SPARE], F32, name=f"plow{t}", align_bytes=64)
+        plow = keep.tile([P, R + WIDE], F32, name="plow", align_bytes=64)
+        nc.gpsimd.memset(plow[:, 2 * R :], 0.0)
+        plow_late = [keep.tile([P, S + SPARE], F32, name=f"plow{t}", align_bytes=64) for t in (2, 3)]
+        for window in plow_late:
             nc.gpsimd.memset(window[:, R:], 0.0)
-            plow.append(window)
 
         e_codes = keep.tile([P, R], U32, name="e_codes", align_bytes=64)
         e_plane = keep.tile([P, R], U8, name="e_plane", align_bytes=64)
@@ -87,81 +88,79 @@ def tile_picked_ybackof_prob_p_kernel(
 
         by_low = keep.tile([P, R], F32, name="by_low", align_bytes=64)
         by_offs = keep.tile([P, S], F32, name="by_offs", align_bytes=64)
-        nc.vector.tensor_copy(by_low[:], rows[:].indirect(low_sb[:]))
         nc.vector.tensor_copy(by_offs[:], rows[:].indirect(offs_sb[:]))
-
-        low_turned = psum.tile([P, 2, P], F32, name="low_turned", tag="bank_y1")
-        for c in range(2):
-            nc.tensor.transpose(low_turned[:, c, :], by_low[:, c * P : (c + 1) * P], ident[:])
-        inv_totl = keep.tile([P, 2], F32, name="inv_totl")
-        nc.vector.reciprocal(inv_totl[:], low_turned[:, :, TOTL_ROW])
-        inv_totl_row = psum.tile([P, R], F32, name="inv_totl_row", tag="bank_r")
-        for c in range(2):
-            nc.tensor.transpose(
-                inv_totl_row[:, c * P : (c + 1) * P], inv_totl[:, c : c + 1].to_broadcast([P, P]), ident[:]
-            )
+        nc.vector.tensor_copy(by_low[:], rows[:].indirect(low_sb[:]))
 
         offs_turned = psum.tile([P, 4, P], F32, name="offs_turned", tag="bank_y0")
         for c in range(4):
             nc.tensor.transpose(offs_turned[:, c, :], by_offs[:, c * P : (c + 1) * P], ident[:])
-        inv_tot = keep.tile([P, 4], F32, name="inv_tot")
-        nc.vector.reciprocal(inv_tot[:], offs_turned[:, :, TOT_ROW])
-        bow100 = keep.tile([P, 4], F32, name="bow100")
-        nc.scalar.mul(bow100[:], offs_turned[:, :, BOW_ROW], 100.0)
-        gain = keep.tile([P, 4], F32, name="gain")
-        nc.scalar.mul(gain[:], inv_tot[:], 100.0)
-        shift = keep.tile([P, 4], F32, name="shift")
-        nc.scalar.mul(shift[:], inv_tot[:], -75.0)
-        bow_bank = psum.tile([P, S], F32, name="bow_bank", tag="bank_y1")
-        for c in range(4):
-            nc.tensor.transpose(
-                bow_bank[:, c * P : (c + 1) * P], bow100[:, c : c + 1].to_broadcast([P, P]), ident[:]
-            )
-        bow_row = keep.tile([P, S], F32, name="bow_row", align_bytes=64)
-        nc.scalar.copy(bow_row[:], bow_bank[:])
-
+        low_turned = psum.tile([P, 2, P], F32, name="low_turned", tag="bank_y1")
+        for c in range(2):
+            nc.tensor.transpose(low_turned[:, c, :], by_low[:, c * P : (c + 1) * P], ident[:])
         h_codes = keep.tile([P, V], U32, name="h_codes", align_bytes=64)
         h_plane = keep.tile([P, V], U8, name="h_plane", align_bytes=64)
-        for t in range(4):
-            cols = slice(t * P, (t + 1) * P)
-            grouped = keep.tile([P, P, PACK], BF16, name=f"grouped{t}", align_bytes=64)
-            src = h_raw[t // 2][:, :, (t % 2) * P : (t % 2 + 1) * P]
+
+        def quantise(half):
+            cols = slice(half * HALF, (half + 1) * HALF)
+            grouped = keep.tile([P, HALF, PACK], BF16, name=f"grouped{half}", tag=f"grouped{half}", align_bytes=64)
             nc.scalar.copy(
                 grouped[:].rearrange("p (c i) j -> p c j i", i=4),
-                src.rearrange("p j (c i) -> p c j i", i=4),
+                h_raw[half][:].rearrange("p j (c i) -> p c j i", i=4),
             )
             nc.vector.quantize_mx(
                 out=h_codes[:, cols].bitcast(FP8X4),
                 scales=h_plane[:, cols],
                 in_=grouped[:].rearrange("p c j -> p (c j)"),
             )
-        for t in range(4):
-            cols = slice(t * P, (t + 1) * P)
-            z_bank = psum.tile([P, R], F32, name=f"z_bank{t}", tag="bank_z")
-            nc.tensor.matmul_mx(
-                out=z_bank[:],
-                lhsT=h_codes[:, cols].bitcast(FP8X4),
-                lhsT_scale=h_plane[:, cols],
-                rhs=e_codes[:].bitcast(FP8X4),
-                rhs_scale=e_plane[:],
-                start=True,
-                stop=True,
+
+        def low_order(half, counts_low):
+            z_bank = psum.tile([P, 2, R], F32, name=f"z_bank{half}", tag="bank_z")
+            for u in range(2):
+                t = 2 * half + 1 - u
+                nc.tensor.matmul_mx(
+                    out=z_bank[:, u, :],
+                    lhsT=h_codes[:, t * P : (t + 1) * P].bitcast(FP8X4),
+                    lhsT_scale=h_plane[:, t * P : (t + 1) * P],
+                    rhs=e_codes[:].bitcast(FP8X4),
+                    rhs_scale=e_plane[:],
+                    start=True,
+                    stop=True,
+                )
+            nc.scalar.activation(counts_low, z_bank[:].rearrange("p u g -> p (u g)"), ACT.Exp, scale=0.8)
+
+        quantise(0)
+        columns = keep.tile([P, 10], F32, name="columns", tag="h_raw0", align_bytes=64)
+        totals, bow100 = columns[:, 0:6], columns[:, 6:10]
+        nc.scalar.copy(totals[:, 0:4], offs_turned[:, :, TOT_ROW])
+        nc.scalar.mul(bow100, offs_turned[:, :, BOW_ROW], 100.0)
+        nc.scalar.copy(totals[:, 4:6], low_turned[:, :, TOTL_ROW])
+        inverse = keep.tile([P, 6], F32, name="inverse")
+        nc.vector.reciprocal(inverse[:], totals)
+        gain = keep.tile([P, 4], F32, name="gain")
+        nc.gpsimd.tensor_scalar(gain[:], inverse[:, 0:4], 100.0, 0.0, ALU.mult, ALU.add)
+        shift = keep.tile([P, 4], F32, name="shift")
+        nc.gpsimd.tensor_scalar(shift[:], inverse[:, 0:4], -75.0, 0.0, ALU.mult, ALU.add)
+        bow_bank = psum.tile([P, S], F32, name="bow_bank", tag="bank_y0")
+        for c in range(4):
+            nc.tensor.transpose(
+                bow_bank[:, c * P : (c + 1) * P], bow100[:, c : c + 1].to_broadcast([P, P]), ident[:]
             )
-            counts_low = keep.tile([P, R], F32, name=f"counts_low{t}", align_bytes=64)
-            nc.scalar.activation(counts_low[:], z_bank[:], ACT.Exp, scale=0.8)
-            nc.vector.tensor_tensor(plow[t][:, 0:R], counts_low[:], inv_totl_row[:], ALU.mult)
+        inv_totl_row = psum.tile([P, R], F32, name="inv_totl_row", tag="bank_r")
+        for c in range(2):
+            nc.tensor.transpose(
+                inv_totl_row[:, c * P : (c + 1) * P], inverse[:, 4 + c : 5 + c].to_broadcast([P, P]), ident[:]
+            )
 
         out_banks = [psum.tile([P, S], F32, name=f"out_bank{t}", tag=f"bank_o{t}") for t in range(4)]
-        for t in range(4):
+
+        def add_turned(t, c, source, start, stop):
+            nc.tensor.matmul(
+                out_banks[t][:, c * P : (c + 1) * P], source, ident[:], start=start, stop=stop, is_transpose=True
+            )
+
+        for t in (2, 3):
             for c in range(4):
-                nc.tensor.matmul(
-                    out_banks[t][:, c * P : (c + 1) * P],
-                    shift[:, c : c + 1].to_broadcast([P, P]),
-                    ident[:],
-                    start=(c == 0),
-                    stop=False,
-                    is_transpose=True,
-                )
+                add_turned(t, c, shift[:, c : c + 1].to_broadcast([P, P]), c == 0, False)
 
         x_codes = keep.tile([P, S], U32, name="x_codes", align_bytes=64)
         x_plane = keep.tile([P, S], U8, name="x_plane", align_bytes=64)
@@ -171,18 +170,46 @@ def tile_picked_ybackof_prob_p_kernel(
             nc.vector.tensor_copy(x_codes[:, cols], x_word_tab[:].indirect(piece))
             nc.vector.tensor_copy(x_plane[:, cols], x_scale_tab[:].indirect(piece))
 
-        def gather_backoff(t, term):
-            for h in range(2):
-                cols = slice(h * HALF, (h + 1) * HALF)
-                nc.vector.tensor_tensor(
-                    term[:, cols],
-                    plow[t][:].indirect(suf_sb[:, h * 16 : (h + 1) * 16]),
-                    bow_row[:, cols],
-                    ALU.mult,
-                )
+        quantise(1)
+        after_h = keep.tile([P, 2 * S], F32, name="after_h", tag="h_raw1", align_bytes=64)
+        counts_low, bow_row = after_h[:, 0:S], after_h[:, S:]
+        low_order(0, counts_low)
+        nc.scalar.copy(bow_row, bow_bank[:])
+        nc.vector.tensor_tensor(
+            plow[:, 0 : 2 * R].rearrange("p (u g) -> p u g", u=2),
+            counts_low.rearrange("p (u g) -> p u g", u=2),
+            inv_totl_row[:].unsqueeze(1).to_broadcast([P, 2, R]),
+            ALU.mult,
+        )
 
-        early = keep.tile([P, 2 * S], F32, name="backoff01", tag="x_words_then_backoff", align_bytes=64)
-        backoff = [early[:, 0:S], early[:, S:]]
+        def fetch(t, tag):
+            picked = keep.tile([P, S], F32, name=f"picked{t}", tag=tag, align_bytes=64)
+            first = (1 - t) * R
+            nc.vector.tensor_copy(picked[:], plow[:, first : first + WIDE].indirect(suf_sb[:]))
+            return picked
+
+        picked = [fetch(0, "grouped1")]
+        counts_late = keep.tile([P, S], F32, name="counts_late", align_bytes=64)
+        low_order(1, counts_late[:])
+        nc.vector.tensor_tensor(plow_late[0][:, 0:R], counts_late[:, R:], inv_totl_row[:], ALU.mult)
+        nc.vector.tensor_tensor(plow_late[1][:, 0:R], counts_late[:, 0:R], inv_totl_row[:], ALU.mult)
+        def add_backoff(t, tag, stop):
+            turned = psum.tile([P, 4, P], F32, name=f"turned{t}", tag=tag)
+            for c in range(4):
+                nc.tensor.transpose(turned[:, c, :], picked[t][:, c * P : (c + 1) * P], ident[:])
+            weighted = keep.tile([P, 4, P], F32, name=f"weighted{t}", align_bytes=64)
+            for c in range(4):
+                nc.scalar.activation(
+                    weighted[:, c, :],
+                    turned[:, c, :],
+                    ACT.Identity,
+                    scale=bow100[:, c : c + 1],
+                    bias=shift[:, c : c + 1],
+                )
+            for c in range(4):
+                add_turned(t, c, weighted[:, c, :], not stop and c == 0, stop and c == 3)
+
+        scaled = []
         for c in range(4):
             cols = slice(c * P, (c + 1) * P)
             y_bank = psum.tile([P, V], F32, name=f"y_bank{c}", tag=f"bank_y{c % 2}")
@@ -197,26 +224,33 @@ def tile_picked_ybackof_prob_p_kernel(
             )
             counts = keep.tile([P, V], F32, name=f"counts{c}", tag=f"counts{c}", align_bytes=64)
             nc.scalar.activation(counts[:], y_bank[:], ACT.Exp, scale=0.8)
-            if c % 2 == 0:
-                gather_backoff(c // 2, backoff[c // 2])
-            scaled = keep.tile([P, V], F32, name=f"scaled{c}", align_bytes=64)
-            nc.vector.tensor_scalar(scaled[:], counts[:], 0.75, gain[:, c : c + 1], ALU.max, ALU.mult)
-            for t in range(4):
-                nc.tensor.matmul(
-                    out_banks[t][:, cols],
-                    scaled[:, t * P : (t + 1) * P],
-                    ident[:],
-                    start=False,
-                    stop=(c == 3),
-                    is_transpose=True,
-                )
-            if c % 2 == 1:
-                late = keep.tile([P, S], F32, name=f"backoff{2 + c // 2}", tag=f"counts{c}", align_bytes=64)
-                backoff.append(late[:])
-        for t in (2, 3):
-            gather_backoff(t, backoff[t])
+            kept = keep.tile([P, V], F32, name=f"scaled{c}", align_bytes=64)
+            nc.vector.tensor_scalar(kept[:], counts[:], 0.75, gain[:, c : c + 1], ALU.max, ALU.mult)
+            scaled.append(kept)
+            if c == 1:
+                picked.append(fetch(1, f"counts{c}"))
 
-        for t in range(4):
+        add_backoff(0, "bank_r", False)
+        for c in range(4):
+            for t in range(4):
+                add_turned(t, c, scaled[c][:, t * P : (t + 1) * P], t == 1 and c == 0, t != 1 and c == 3)
+        add_backoff(1, "bank_z", True)
+        for t in range(2):
             result = keep.tile([P, S], F32, name=f"result{t}", align_bytes=64)
-            nc.vector.tensor_tensor(result[:], out_banks[t][:], backoff[t], ALU.add)
+            nc.scalar.copy(result[:], out_banks[t][:])
             nc.sync.dma_start(out[t * P : (t + 1) * P, :], result[:])
+
+        backoff = keep.tile([P, 2 * S], F32, name="backoff", tag="counts3", align_bytes=64)
+        for u in range(2):
+            nc.vector.tensor_tensor(
+                backoff[:, u * S : (u + 1) * S], plow_late[u][:].indirect(suf_sb[:]), bow_row, ALU.mult
+            )
+
+        for t, pieces in ((2, 1), (3, 2)):
+            result = keep.tile([P, S], F32, name=f"result{t}", align_bytes=64)
+            width = S // pieces
+            for first in range(0, S, width):
+                cols = slice(first, first + width)
+                term = backoff[:, (t - 2) * S + first : (t - 2) * S + first + width]
+                nc.vector.tensor_tensor(result[:, cols], out_banks[t][:, cols], term, ALU.add)
+                nc.sync.dma_start(out[t * P : (t + 1) * P, cols], result[:, cols])

@@ -1,3 +1,4 @@
+import math
 from contextlib import ExitStack
 
 import concourse.mybir as mybir
@@ -6,8 +7,9 @@ from concourse.masks import make_identity
 K, T, S, V, R, W = 512, 2048, 512, 512, 256, 1024
 P = 128
 PACK = 4
+PER_COLUMN = 16
 FLOPS = 2 * K * V * (S + R)
-BYTES = K * (T + W) + (K // 32) * (T + W) + 4 * K * V + 4 * (2 * T + W) + 2 * P * (2 * S + R) // 16 + 4 * V * S
+BYTES = (K + K // 32) * (T + W) + 4 * K * V + 4 * (2 * T + W) + 2 * P * (2 * S + R) // PER_COLUMN + 4 * V * S
 
 F32 = mybir.dt.float32
 BF16 = mybir.dt.bfloat16
@@ -20,9 +22,9 @@ ALU = mybir.AluOpType
 ACT = mybir.ActivationFunctionType
 
 TOT_ROW, BOW_ROW, TOTL_ROW = 4, 8, 12
-HALF = 256
-SPARE = 16
-WIDE = 704
+HALF = V // 2
+COPY_WINDOW = 704
+MULT_WINDOW = S + 16
 
 
 def tile_picked_ybackof_prob_p_kernel(
@@ -33,20 +35,26 @@ def tile_picked_ybackof_prob_p_kernel(
         keep = ctx.enter_context(tc.tile_pool(name="keep", bufs=1))
         psum = ctx.enter_context(tc.psum_pool(name="psum", bufs=1))
 
-        low_sb = keep.tile([P, R // 16], U16, name="low_sb")
-        offs_sb = keep.tile([P, S // 16], U16, name="offs_sb")
-        suf_sb = keep.tile([P, S // 16], U16, name="suf_sb")
+        low_sb = keep.tile([P, R // PER_COLUMN], U16, name="low_sb")
+        offs_sb = keep.tile([P, S // PER_COLUMN], U16, name="offs_sb")
+        suf_sb = keep.tile([P, S // PER_COLUMN], U16, name="suf_sb")
         e_scale_tab = keep.tile([P, W], U8, name="e_scale_tab", align_bytes=64)
         x_scale_tab = keep.tile([P, T], U8, name="x_scale_tab", align_bytes=64)
+        e_word_tab = keep.tile([P, W], U32, name="e_word_tab", align_bytes=64)
+        x_word_tab = keep.tile([P, T], U32, name="x_word_tab", align_bytes=64)
         rows = keep.tile([P, T], F32, name="rows", align_bytes=64)
+        h_raw = [
+            keep.tile([P, PACK, HALF], F32, name=f"h_raw{half}", tag=f"h_raw{half}", align_bytes=64)
+            for half in range(2)
+        ]
+
+        nc.gpsimd.memset(rows[:, 0 : T // 2], 0.0)
+        nc.vector.memset(rows[:, T // 2 :], 0.0)
         nc.vector.memset(e_scale_tab[:].bitcast(I32), 0)
-        nc.vector.memset(rows[:], 0.0)
         nc.vector.memset(x_scale_tab[:].bitcast(I32), 0)
 
         ident = keep.tile([P, P], F32, name="ident", align_bytes=64)
         make_identity(nc, ident[:])
-        warm = keep.tile([P, 1], F32, name="warm")
-        nc.scalar.activation(warm[:], ident[:, 0:1], ACT.Exp)
 
         def load_scale_rows(table, scales):
             for q in range(4):
@@ -55,48 +63,70 @@ def tile_picked_ybackof_prob_p_kernel(
                 )
 
         def load_words(table, words):
-            nc.sync.dma_start(table[:].bitcast(I32), words[0].rearrange("p n t -> p (n t)").bitcast(I32))
+            nc.sync.dma_start(table[:].bitcast(I32), words[0].rearrange("p n j -> p (n j)").bitcast(I32))
 
-        e_word_tab = keep.tile([P, W], U32, name="e_word_tab", align_bytes=64)
-        x_word_tab = keep.tile([P, T], U32, name="x_word_tab", align_bytes=64)
-        h_raw = [keep.tile([P, PACK, HALF], F32, name=f"h_raw{c}", tag=f"h_raw{c}", align_bytes=64) for c in range(2)]
         h_rows = hT.rearrange("(p j) t -> p j t", j=PACK)
-
         load_words(e_word_tab, e_words)
         nc.sync.dma_start(low_sb[:], low)
-        load_scale_rows(e_scale_tab, e_scales)
         nc.sync.dma_start(offs_sb[:], offs)
-        nc.sync.dma_start(h_raw[0][:], h_rows[:, :, 0:HALF])
+        nc.sync.dma_start(rows[TOTL_ROW : TOTL_ROW + 1, 0:W], totl[0:1, :])
         nc.sync.dma_start(rows[TOT_ROW : TOT_ROW + 1, :], tot[0:1, :])
         nc.sync.dma_start(rows[BOW_ROW : BOW_ROW + 1, :], bow[0:1, :])
-        nc.sync.dma_start(rows[TOTL_ROW : TOTL_ROW + 1, 0:W], totl[0:1, :])
         load_words(x_word_tab, x_words)
+        load_scale_rows(e_scale_tab, e_scales)
+        nc.sync.dma_start(h_raw[0][:], h_rows[:, :, 0:HALF])
         load_scale_rows(x_scale_tab, x_scales)
         nc.sync.dma_start(h_raw[1][:], h_rows[:, :, HALF:])
         nc.sync.dma_start(suf_sb[:], suf)
 
-        plow = keep.tile([P, R + WIDE], F32, name="plow", align_bytes=64)
-        nc.gpsimd.memset(plow[:, 2 * R :], 0.0)
-        plow_late = [keep.tile([P, S + SPARE], F32, name=f"plow{t}", align_bytes=64) for t in (2, 3)]
+        plow_early = keep.tile([P, R + COPY_WINDOW], F32, name="plow_early", align_bytes=64)
+        nc.gpsimd.memset(plow_early[:, 2 * R :], 0.0)
+        plow_late = [keep.tile([P, MULT_WINDOW], F32, name=f"plow{t}", align_bytes=64) for t in (2, 3)]
         for window in plow_late:
             nc.gpsimd.memset(window[:, R:], 0.0)
 
         e_codes = keep.tile([P, R], U32, name="e_codes", align_bytes=64)
         e_plane = keep.tile([P, R], U8, name="e_plane", align_bytes=64)
         nc.vector.tensor_copy(e_codes[:], e_word_tab[:].indirect(low_sb[:]))
-        nc.vector.tensor_copy(e_plane[:], e_scale_tab[:].indirect(low_sb[:]))
+
+        def turn(bank, source, blocks):
+            for c in range(blocks):
+                nc.tensor.transpose(bank[:, c, :], source[:, c * P : (c + 1) * P], ident[:])
+
+        def spread(bank, columns, blocks):
+            for c in range(blocks):
+                nc.tensor.transpose(
+                    bank[:, c * P : (c + 1) * P], columns[:, c : c + 1].to_broadcast([P, P]), ident[:]
+                )
 
         by_low = keep.tile([P, R], F32, name="by_low", align_bytes=64)
         by_offs = keep.tile([P, S], F32, name="by_offs", align_bytes=64)
-        nc.vector.tensor_copy(by_offs[:], rows[:].indirect(offs_sb[:]))
         nc.vector.tensor_copy(by_low[:], rows[:].indirect(low_sb[:]))
+        nc.vector.tensor_copy(by_offs[:], rows[:].indirect(offs_sb[:]))
+        low_turned = psum.tile([P, R // P, P], F32, name="low_turned", tag="bank_out1")
+        turn(low_turned, by_low, R // P)
+        inv_totl = keep.tile([P, R // P], F32, name="inv_totl")
+        nc.vector.reciprocal(inv_totl[:], low_turned[:, :, TOTL_ROW])
+        inv_totl_row = psum.tile([P, R], F32, name="inv_totl_row", tag="bank_row")
+        spread(inv_totl_row, inv_totl, R // P)
 
-        offs_turned = psum.tile([P, 4, P], F32, name="offs_turned", tag="bank_y0")
-        for c in range(4):
-            nc.tensor.transpose(offs_turned[:, c, :], by_offs[:, c * P : (c + 1) * P], ident[:])
-        low_turned = psum.tile([P, 2, P], F32, name="low_turned", tag="bank_y1")
-        for c in range(2):
-            nc.tensor.transpose(low_turned[:, c, :], by_low[:, c * P : (c + 1) * P], ident[:])
+        offs_turned = psum.tile([P, S // P, P], F32, name="offs_turned", tag="bank_out0")
+        turn(offs_turned, by_offs, S // P)
+        totals = keep.tile([P, S // P], F32, name="totals")
+        nc.scalar.copy(totals[:], offs_turned[:, :, TOT_ROW])
+        bow100 = keep.tile([P, S // P], F32, name="bow100")
+        nc.scalar.mul(bow100[:], offs_turned[:, :, BOW_ROW], 100.0)
+        inv_tot = keep.tile([P, S // P], F32, name="inv_tot")
+        nc.vector.reciprocal(inv_tot[:], totals[:])
+        shift = keep.tile([P, S // P], F32, name="shift")
+        nc.gpsimd.tensor_scalar(shift[:], inv_tot[:], -75.0, 0.0, ALU.mult, ALU.add)
+
+        nc.vector.tensor_copy(e_plane[:], e_scale_tab[:].indirect(low_sb[:]))
+        x_codes = keep.tile([P, S], U32, name="x_codes", align_bytes=64)
+        x_plane = keep.tile([P, S], U8, name="x_plane", align_bytes=64)
+        nc.vector.tensor_copy(x_codes[:], x_word_tab[:].indirect(offs_sb[:]))
+        nc.vector.tensor_copy(x_plane[:], x_scale_tab[:].indirect(offs_sb[:]))
+
         h_codes = keep.tile([P, V], U32, name="h_codes", align_bytes=64)
         h_plane = keep.tile([P, V], U8, name="h_plane", align_bytes=64)
 
@@ -113,12 +143,12 @@ def tile_picked_ybackof_prob_p_kernel(
                 in_=grouped[:].rearrange("p c j -> p (c j)"),
             )
 
-        def low_order(half, counts_low):
+        def suffix_counts(half, exp_z):
             z_bank = psum.tile([P, 2, R], F32, name=f"z_bank{half}", tag="bank_z")
-            for u in range(2):
-                t = 2 * half + 1 - u
+            for place in range(2):
+                t = 2 * half + 1 - place
                 nc.tensor.matmul_mx(
-                    out=z_bank[:, u, :],
+                    out=z_bank[:, place, :],
                     lhsT=h_codes[:, t * P : (t + 1) * P].bitcast(FP8X4),
                     lhsT_scale=h_plane[:, t * P : (t + 1) * P],
                     rhs=e_codes[:].bitcast(FP8X4),
@@ -126,91 +156,41 @@ def tile_picked_ybackof_prob_p_kernel(
                     start=True,
                     stop=True,
                 )
-            nc.scalar.activation(counts_low, z_bank[:].rearrange("p u g -> p (u g)"), ACT.Exp, scale=0.8)
+            nc.scalar.activation(exp_z, z_bank[:].rearrange("p u g -> p (u g)"), ACT.Exp, scale=0.8)
 
         quantise(0)
-        columns = keep.tile([P, 10], F32, name="columns", tag="h_raw0", align_bytes=64)
-        totals, bow100 = columns[:, 0:6], columns[:, 6:10]
-        nc.scalar.copy(totals[:, 0:4], offs_turned[:, :, TOT_ROW])
-        nc.scalar.mul(bow100, offs_turned[:, :, BOW_ROW], 100.0)
-        nc.scalar.copy(totals[:, 4:6], low_turned[:, :, TOTL_ROW])
-        inverse = keep.tile([P, 6], F32, name="inverse")
-        nc.vector.reciprocal(inverse[:], totals)
-        gain = keep.tile([P, 4], F32, name="gain")
-        nc.gpsimd.tensor_scalar(gain[:], inverse[:, 0:4], 100.0, 0.0, ALU.mult, ALU.add)
-        shift = keep.tile([P, 4], F32, name="shift")
-        nc.gpsimd.tensor_scalar(shift[:], inverse[:, 0:4], -75.0, 0.0, ALU.mult, ALU.add)
-        bow_bank = psum.tile([P, S], F32, name="bow_bank", tag="bank_y0")
-        for c in range(4):
-            nc.tensor.transpose(
-                bow_bank[:, c * P : (c + 1) * P], bow100[:, c : c + 1].to_broadcast([P, P]), ident[:]
-            )
-        inv_totl_row = psum.tile([P, R], F32, name="inv_totl_row", tag="bank_r")
-        for c in range(2):
-            nc.tensor.transpose(
-                inv_totl_row[:, c * P : (c + 1) * P], inverse[:, 4 + c : 5 + c].to_broadcast([P, P]), ident[:]
-            )
-
-        out_banks = [psum.tile([P, S], F32, name=f"out_bank{t}", tag=f"bank_o{t}") for t in range(4)]
-
-        def add_turned(t, c, source, start, stop):
-            nc.tensor.matmul(
-                out_banks[t][:, c * P : (c + 1) * P], source, ident[:], start=start, stop=stop, is_transpose=True
-            )
-
-        for t in (2, 3):
-            for c in range(4):
-                add_turned(t, c, shift[:, c : c + 1].to_broadcast([P, P]), c == 0, False)
-
-        x_codes = keep.tile([P, S], U32, name="x_codes", align_bytes=64)
-        x_plane = keep.tile([P, S], U8, name="x_plane", align_bytes=64)
-        for h in range(2):
-            cols = slice(h * HALF, (h + 1) * HALF)
-            piece = offs_sb[:, h * 16 : (h + 1) * 16]
-            nc.vector.tensor_copy(x_codes[:, cols], x_word_tab[:].indirect(piece))
-            nc.vector.tensor_copy(x_plane[:, cols], x_scale_tab[:].indirect(piece))
-
         quantise(1)
-        after_h = keep.tile([P, 2 * S], F32, name="after_h", tag="h_raw1", align_bytes=64)
-        counts_low, bow_row = after_h[:, 0:S], after_h[:, S:]
-        low_order(0, counts_low)
+
+        bow_bank = psum.tile([P, S], F32, name="bow_bank", tag="bank_out1")
+        spread(bow_bank, bow100, S // P)
+        after_h = keep.tile([P, 2 * R + S], F32, name="after_h", tag="h_raw1", align_bytes=64)
+        exp_z_early, bow_row = after_h[:, 0 : 2 * R], after_h[:, 2 * R :]
+        suffix_counts(0, exp_z_early)
         nc.scalar.copy(bow_row, bow_bank[:])
         nc.vector.tensor_tensor(
-            plow[:, 0 : 2 * R].rearrange("p (u g) -> p u g", u=2),
-            counts_low.rearrange("p (u g) -> p u g", u=2),
+            plow_early[:, 0 : 2 * R].rearrange("p (u g) -> p u g", u=2),
+            exp_z_early.rearrange("p (u g) -> p u g", u=2),
             inv_totl_row[:].unsqueeze(1).to_broadcast([P, 2, R]),
             ALU.mult,
         )
 
         def fetch(t, tag):
-            picked = keep.tile([P, S], F32, name=f"picked{t}", tag=tag, align_bytes=64)
+            fetched = keep.tile([P, S], F32, name=f"fetched{t}", tag=tag, align_bytes=64)
             first = (1 - t) * R
-            nc.vector.tensor_copy(picked[:], plow[:, first : first + WIDE].indirect(suf_sb[:]))
-            return picked
+            nc.vector.tensor_copy(fetched[:], plow_early[:, first : first + COPY_WINDOW].indirect(suf_sb[:]))
+            return fetched
 
         picked = [fetch(0, "grouped1")]
-        counts_late = keep.tile([P, S], F32, name="counts_late", align_bytes=64)
-        low_order(1, counts_late[:])
-        nc.vector.tensor_tensor(plow_late[0][:, 0:R], counts_late[:, R:], inv_totl_row[:], ALU.mult)
-        nc.vector.tensor_tensor(plow_late[1][:, 0:R], counts_late[:, 0:R], inv_totl_row[:], ALU.mult)
-        def add_backoff(t, tag, stop):
-            turned = psum.tile([P, 4, P], F32, name=f"turned{t}", tag=tag)
-            for c in range(4):
-                nc.tensor.transpose(turned[:, c, :], picked[t][:, c * P : (c + 1) * P], ident[:])
-            weighted = keep.tile([P, 4, P], F32, name=f"weighted{t}", align_bytes=64)
-            for c in range(4):
-                nc.scalar.activation(
-                    weighted[:, c, :],
-                    turned[:, c, :],
-                    ACT.Identity,
-                    scale=bow100[:, c : c + 1],
-                    bias=shift[:, c : c + 1],
-                )
-            for c in range(4):
-                add_turned(t, c, weighted[:, c, :], not stop and c == 0, stop and c == 3)
+        exp_z_late = keep.tile([P, 2 * R], F32, name="exp_z_late", align_bytes=64)
+        suffix_counts(1, exp_z_late[:])
+        for t in (2, 3):
+            first = (3 - t) * R
+            nc.vector.tensor_tensor(
+                plow_late[t - 2][:, 0:R], exp_z_late[:, first : first + R], inv_totl_row[:], ALU.mult
+            )
 
         scaled = []
-        for c in range(4):
+        for c in range(S // P):
             cols = slice(c * P, (c + 1) * P)
             y_bank = psum.tile([P, V], F32, name=f"y_bank{c}", tag=f"bank_y{c % 2}")
             nc.tensor.matmul_mx(
@@ -222,28 +202,60 @@ def tile_picked_ybackof_prob_p_kernel(
                 start=True,
                 stop=True,
             )
-            counts = keep.tile([P, V], F32, name=f"counts{c}", tag=f"counts{c}", align_bytes=64)
-            nc.scalar.activation(counts[:], y_bank[:], ACT.Exp, scale=0.8)
-            kept = keep.tile([P, V], F32, name=f"scaled{c}", align_bytes=64)
-            nc.vector.tensor_scalar(kept[:], counts[:], 0.75, gain[:, c : c + 1], ALU.max, ALU.mult)
-            scaled.append(kept)
+            exp_y = keep.tile([P, V], F32, name=f"exp_y{c}", tag=f"exp_y{c}", align_bytes=64)
+            nc.scalar.activation(exp_y[:], y_bank[:], ACT.Exp, scale=0.8, bias=math.log(100.0))
+            block = keep.tile([P, V], F32, name=f"scaled{c}", align_bytes=64)
+            nc.vector.tensor_scalar(block[:], exp_y[:], 75.0, inv_tot[:, c : c + 1], ALU.max, ALU.mult)
+            scaled.append(block)
             if c == 1:
-                picked.append(fetch(1, f"counts{c}"))
+                picked.append(fetch(1, "exp_y1"))
 
-        add_backoff(0, "bank_r", False)
-        for c in range(4):
-            for t in range(4):
-                add_turned(t, c, scaled[c][:, t * P : (t + 1) * P], t == 1 and c == 0, t != 1 and c == 3)
-        add_backoff(1, "bank_z", True)
-        for t in range(2):
+        out_banks = [psum.tile([P, S], F32, name=f"out_bank{t}", tag=f"bank_out{t}") for t in range(V // P)]
+
+        def add_turned(t, c, source, start, stop):
+            nc.tensor.matmul(
+                out_banks[t][:, c * P : (c + 1) * P], source, ident[:], start=start, stop=stop, is_transpose=True
+            )
+
+        def add_scaled(c):
+            last = c == S // P - 1
+            for t in range(V // P):
+                add_turned(t, c, scaled[c][:, t * P : (t + 1) * P], t < 2 and c == 0, t >= 2 and last)
+
+        def weigh(t, tag):
+            turned = psum.tile([P, S // P, P], F32, name=f"turned{t}", tag=tag)
+            turn(turned, picked[t], S // P)
+            weighted = keep.tile([P, S // P, P], F32, name=f"weighted{t}", align_bytes=64)
+            for c in range(S // P):
+                nc.scalar.activation(
+                    weighted[:, c, :],
+                    turned[:, c, :],
+                    ACT.Identity,
+                    scale=bow100[:, c : c + 1],
+                    bias=shift[:, c : c + 1],
+                )
+            return weighted
+
+        for t in (2, 3):
+            for c in range(S // P):
+                add_turned(t, c, shift[:, c : c + 1].to_broadcast([P, P]), c == 0, False)
+        weighted = [weigh(0, "bank_z")]
+        add_scaled(0)
+        add_scaled(1)
+        weighted.append(weigh(1, "bank_row"))
+        add_scaled(2)
+        add_scaled(3)
+        for t in (0, 1):
+            for c in range(S // P):
+                add_turned(t, c, weighted[t][:, c, :], False, c == S // P - 1)
             result = keep.tile([P, S], F32, name=f"result{t}", align_bytes=64)
             nc.scalar.copy(result[:], out_banks[t][:])
-            nc.sync.dma_start(out[t * P : (t + 1) * P, :], result[:])
+            nc.scalar.dma_start(out[t * P : (t + 1) * P, :], result[:])
 
-        backoff = keep.tile([P, 2 * S], F32, name="backoff", tag="counts3", align_bytes=64)
-        for u in range(2):
+        backoff = keep.tile([P, 2 * S], F32, name="backoff", tag="exp_y3", align_bytes=64)
+        for t in (2, 3):
             nc.vector.tensor_tensor(
-                backoff[:, u * S : (u + 1) * S], plow_late[u][:].indirect(suf_sb[:]), bow_row, ALU.mult
+                backoff[:, (t - 2) * S : (t - 1) * S], plow_late[t - 2][:].indirect(suf_sb[:]), bow_row, ALU.mult
             )
 
         for t, pieces in ((2, 1), (3, 2)):

@@ -80,10 +80,10 @@ def tile_picked_ybackof_prob_p_kernel(
         nc.sync.dma_start(suf_sb[:], suf)
 
         plow_early = keep.tile([P, R + COPY_WINDOW], F32, name="plow_early", align_bytes=64)
-        nc.gpsimd.memset(plow_early[:, 2 * R :], 0.0)
+        nc.vector.memset(plow_early[:, 2 * R :], 0.0)
         plow_late = [keep.tile([P, MULT_WINDOW], F32, name=f"plow{t}", align_bytes=64) for t in (2, 3)]
         for window in plow_late:
-            nc.gpsimd.memset(window[:, R:], 0.0)
+            nc.vector.memset(window[:, R:], 0.0)
 
         e_codes = keep.tile([P, R], U32, name="e_codes", align_bytes=64)
         e_plane = keep.tile([P, R], U8, name="e_plane", align_bytes=64)
@@ -220,7 +220,7 @@ def tile_picked_ybackof_prob_p_kernel(
         def add_scaled(c):
             last = c == S // P - 1
             for t in range(V // P):
-                add_turned(t, c, scaled[c][:, t * P : (t + 1) * P], t < 2 and c == 0, t >= 2 and last)
+                add_turned(t, c, scaled[c][:, t * P : (t + 1) * P], t < 2 and c == 0, t != 1 and last)
 
         def weigh(t, tag):
             turned = psum.tile([P, S // P, P], F32, name=f"turned{t}", tag=tag)
@@ -236,6 +236,10 @@ def tile_picked_ybackof_prob_p_kernel(
                 )
             return weighted
 
+        def add_weighted(t, closes_group):
+            for c in range(S // P):
+                add_turned(t, c, weighted[t][:, c, :], False, closes_group and c == S // P - 1)
+
         for t in (2, 3):
             for c in range(S // P):
                 add_turned(t, c, shift[:, c : c + 1].to_broadcast([P, P]), c == 0, False)
@@ -244,10 +248,10 @@ def tile_picked_ybackof_prob_p_kernel(
         add_scaled(1)
         weighted.append(weigh(1, "bank_row"))
         add_scaled(2)
+        add_weighted(0, False)
         add_scaled(3)
+        add_weighted(1, True)
         for t in (0, 1):
-            for c in range(S // P):
-                add_turned(t, c, weighted[t][:, c, :], False, c == S // P - 1)
             result = keep.tile([P, S], F32, name=f"result{t}", align_bytes=64)
             nc.scalar.copy(result[:], out_banks[t][:])
             nc.scalar.dma_start(out[t * P : (t + 1) * P, :], result[:])

import math
from contextlib import ExitStack

import concourse.mybir as mybir
from concourse.masks import make_identity

K, T, S, V, R, W = 512, 2048, 512, 512, 256, 1024
P = 128
PACK = 4
PER_COLUMN = 16
FLOPS = 2 * K * V * (S + R)
BYTES = (K + K // 32) * (T + W) + 4 * K * V + 4 * (2 * T + W) + 2 * P * (2 * S + R) // PER_COLUMN + 4 * V * S

F32 = mybir.dt.float32
BF16 = mybir.dt.bfloat16
I32 = mybir.dt.int32
U32 = mybir.dt.uint32
U16 = mybir.dt.uint16
U8 = mybir.dt.uint8
FP8X4 = mybir.dt.float8_e4m3fn_x4
ALU = mybir.AluOpType
ACT = mybir.ActivationFunctionType

TOT_ROW, BOW_ROW, TOTL_ROW = 4, 8, 12
HALF = V // 2
COPY_WINDOW = 704
MULT_WINDOW = S + 16


def tile_picked_ybackof_prob_p_kernel(
    tc, x_words, x_scales, hT, e_words, e_scales, totl, bow, tot, offs, low, suf, out
):
    nc = tc.nc
    with ExitStack() as ctx:
        keep = ctx.enter_context(tc.tile_pool(name="keep", bufs=1))
        psum = ctx.enter_context(tc.psum_pool(name="psum", bufs=1))

        low_sb = keep.tile([P, R // PER_COLUMN], U16, name="low_sb")
        offs_sb = keep.tile([P, S // PER_COLUMN], U16, name="offs_sb")
        suf_sb = keep.tile([P, S // PER_COLUMN], U16, name="suf_sb")
        e_scale_tab = keep.tile([P, W], U8, name="e_scale_tab", align_bytes=64)
        x_scale_tab = keep.tile([P, T], U8, name="x_scale_tab", align_bytes=64)
        e_word_tab = keep.tile([P, W], U32, name="e_word_tab", align_bytes=64)
        x_word_tab = keep.tile([P, T], U32, name="x_word_tab", align_bytes=64)
        rows = keep.tile([P, T], F32, name="rows", align_bytes=64)
        h_raw = [
            keep.tile([P, PACK, HALF], F32, name=f"h_raw{half}", tag=f"h_raw{half}", align_bytes=64)
            for half in range(2)
        ]

        nc.gpsimd.memset(rows[:, 0 : T // 2], 0.0)
        nc.vector.memset(rows[:, T // 2 :], 0.0)
        nc.vector.memset(e_scale_tab[:].bitcast(I32), 0)
        nc.vector.memset(x_scale_tab[:].bitcast(I32), 0)

        ident = keep.tile([P, P], F32, name="ident", align_bytes=64)
        make_identity(nc, ident[:])

        def load_scale_rows(table, scales):
            for q in range(4):
                nc.sync.dma_start(
                    table[32 * q : 32 * q + 4, :].bitcast(I32), scales[0, 4 * q : 4 * q + 4, :].bitcast(I32)
                )

        def load_words(table, words):
            nc.sync.dma_start(table[:].bitcast(I32), words[0].rearrange("p n j -> p (n j)").bitcast(I32))

        h_rows = hT.rearrange("(p j) t -> p j t", j=PACK)
        load_words(e_word_tab, e_words)
        nc.sync.dma_start(low_sb[:], low)
        nc.sync.dma_start(offs_sb[:], offs)
        nc.sync.dma_start(rows[TOTL_ROW : TOTL_ROW + 1, 0:W], totl[0:1, :])
        nc.sync.dma_start(rows[TOT_ROW : TOT_ROW + 1, :], tot[0:1, :])
        nc.sync.dma_start(rows[BOW_ROW : BOW_ROW + 1, :], bow[0:1, :])
        load_words(x_word_tab, x_words)
        load_scale_rows(e_scale_tab, e_scales)
        nc.sync.dma_start(h_raw[0][:], h_rows[:, :, 0:HALF])
        load_scale_rows(x_scale_tab, x_scales)
        nc.sync.dma_start(h_raw[1][:], h_rows[:, :, HALF:])
        nc.sync.dma_start(suf_sb[:], suf)

        plow_early = keep.tile([P, R + COPY_WINDOW], F32, name="plow_early", align_bytes=64)
        nc.vector.memset(plow_early[:, 2 * R :], 0.0)
        plow_late = [keep.tile([P, MULT_WINDOW], F32, name=f"plow{t}", align_bytes=64) for t in (2, 3)]
        for window in plow_late:
            nc.vector.memset(window[:, R:], 0.0)

        e_codes = keep.tile([P, R], U32, name="e_codes", align_bytes=64)
        e_plane = keep.tile([P, R], U8, name="e_plane", align_bytes=64)
        nc.vector.tensor_copy(e_codes[:], e_word_tab[:].indirect(low_sb[:]))

        def turn(bank, source, blocks):
            for c in range(blocks):
                nc.tensor.transpose(bank[:, c, :], source[:, c * P : (c + 1) * P], ident[:])

        def spread(bank, columns, blocks):
            for c in range(blocks):
                nc.tensor.transpose(
                    bank[:, c * P : (c + 1) * P], columns[:, c : c + 1].to_broadcast([P, P]), ident[:]
                )

        by_low = keep.tile([P, R], F32, name="by_low", align_bytes=64)
        by_offs = keep.tile([P, S], F32, name="by_offs", align_bytes=64)
        nc.vector.tensor_copy(by_low[:], rows[:].indirect(low_sb[:]))
        nc.vector.tensor_copy(by_offs[:], rows[:].indirect(offs_sb[:]))
        low_turned = psum.tile([P, R // P, P], F32, name="low_turned", tag="bank_out1")
        turn(low_turned, by_low, R // P)
        inv_totl = keep.tile([P, R // P], F32, name="inv_totl")
        nc.vector.reciprocal(inv_totl[:], low_turned[:, :, TOTL_ROW])
        inv_totl_row = psum.tile([P, R], F32, name="inv_totl_row", tag="bank_row")
        spread(inv_totl_row, inv_totl, R // P)

        offs_turned = psum.tile([P, S // P, P], F32, name="offs_turned", tag="bank_out0")
        turn(offs_turned, by_offs, S // P)
        totals = keep.tile([P, S // P], F32, name="totals")
        nc.scalar.copy(totals[:], offs_turned[:, :, TOT_ROW])
        bow100 = keep.tile([P, S // P], F32, name="bow100")
        nc.scalar.mul(bow100[:], offs_turned[:, :, BOW_ROW], 100.0)
        inv_tot = keep.tile([P, S // P], F32, name="inv_tot")
        nc.vector.reciprocal(inv_tot[:], totals[:])
        shift = keep.tile([P, S // P], F32, name="shift")
        nc.gpsimd.tensor_scalar(shift[:], inv_tot[:], -75.0, 0.0, ALU.mult, ALU.add)

        nc.vector.tensor_copy(e_plane[:], e_scale_tab[:].indirect(low_sb[:]))
        x_codes = keep.tile([P, S], U32, name="x_codes", align_bytes=64)
        x_plane = keep.tile([P, S], U8, name="x_plane", align_bytes=64)
        nc.vector.tensor_copy(x_codes[:], x_word_tab[:].indirect(offs_sb[:]))
        nc.vector.tensor_copy(x_plane[:], x_scale_tab[:].indirect(offs_sb[:]))

        h_codes = keep.tile([P, V], U32, name="h_codes", align_bytes=64)
        h_plane = keep.tile([P, V], U8, name="h_plane", align_bytes=64)

        def quantise(half):
            cols = slice(half * HALF, (half + 1) * HALF)
            grouped = keep.tile([P, HALF, PACK], BF16, name=f"grouped{half}", tag=f"grouped{half}", align_bytes=64)
            nc.scalar.copy(
                grouped[:].rearrange("p (c i) j -> p c j i", i=4),
                h_raw[half][:].rearrange("p j (c i) -> p c j i", i=4),
            )
            nc.vector.quantize_mx(
                out=h_codes[:, cols].bitcast(FP8X4),
                scales=h_plane[:, cols],
                in_=grouped[:].rearrange("p c j -> p (c j)"),
            )

        def suffix_counts(half, exp_z):
            z_bank = psum.tile([P, 2, R], F32, name=f"z_bank{half}", tag="bank_z")
            for place in range(2):
                t = 2 * half + 1 - place
                nc.tensor.matmul_mx(
                    out=z_bank[:, place, :],
                    lhsT=h_codes[:, t * P : (t + 1) * P].bitcast(FP8X4),
                    lhsT_scale=h_plane[:, t * P : (t + 1) * P],
                    rhs=e_codes[:].bitcast(FP8X4),
                    rhs_scale=e_plane[:],
                    start=True,
                    stop=True,
                )
            nc.scalar.activation(exp_z, z_bank[:].rearrange("p u g -> p (u g)"), ACT.Exp, scale=0.8)

        quantise(0)
        quantise(1)

        bow_bank = psum.tile([P, S], F32, name="bow_bank", tag="bank_out1")
        spread(bow_bank, bow100, S // P)
        after_h = keep.tile([P, 2 * R + S], F32, name="after_h", tag="h_raw1", align_bytes=64)
        exp_z_early, bow_row = after_h[:, 0 : 2 * R], after_h[:, 2 * R :]
        suffix_counts(0, exp_z_early)
        nc.scalar.copy(bow_row, bow_bank[:])
        nc.vector.tensor_tensor(
            plow_early[:, 0 : 2 * R].rearrange("p (u g) -> p u g", u=2),
            exp_z_early.rearrange("p (u g) -> p u g", u=2),
            inv_totl_row[:].unsqueeze(1).to_broadcast([P, 2, R]),
            ALU.mult,
        )

        def fetch(t, tag):
            fetched = keep.tile([P, S], F32, name=f"fetched{t}", tag=tag, align_bytes=64)
            first = (1 - t) * R
            nc.vector.tensor_copy(fetched[:], plow_early[:, first : first + COPY_WINDOW].indirect(suf_sb[:]))
            return fetched

        picked = [fetch(0, "grouped1")]
        exp_z_late = keep.tile([P, 2 * R], F32, name="exp_z_late", align_bytes=64)
        suffix_counts(1, exp_z_late[:])
        for t in (2, 3):
            first = (3 - t) * R
            nc.vector.tensor_tensor(
                plow_late[t - 2][:, 0:R], exp_z_late[:, first : first + R], inv_totl_row[:], ALU.mult
            )

        scaled = []
        for c in range(S // P):
            cols = slice(c * P, (c + 1) * P)
            y_bank = psum.tile([P, V], F32, name=f"y_bank{c}", tag=f"bank_y{c % 2}")
            nc.tensor.matmul_mx(
                out=y_bank[:],
                lhsT=x_codes[:, cols].bitcast(FP8X4),
                lhsT_scale=x_plane[:, cols],
                rhs=h_codes[:].bitcast(FP8X4),
                rhs_scale=h_plane[:],
                start=True,
                stop=True,
            )
            exp_y = keep.tile([P, V], F32, name=f"exp_y{c}", tag=f"exp_y{c}", align_bytes=64)
            nc.scalar.activation(exp_y[:], y_bank[:], ACT.Exp, scale=0.8, bias=math.log(100.0))
            block = keep.tile([P, V], F32, name=f"scaled{c}", align_bytes=64)
            nc.vector.tensor_scalar(block[:], exp_y[:], 75.0, inv_tot[:, c : c + 1], ALU.max, ALU.mult)
            scaled.append(block)
            if c == 1:
                picked.append(fetch(1, "exp_y1"))

        out_banks = [psum.tile([P, S], F32, name=f"out_bank{t}", tag=f"bank_out{t}") for t in range(V // P)]

        def add_turned(t, c, source, start, stop):
            nc.tensor.matmul(
                out_banks[t][:, c * P : (c + 1) * P], source, ident[:], start=start, stop=stop, is_transpose=True
            )

        def add_scaled(c):
            last = c == S // P - 1
            for t in range(V // P):
                add_turned(t, c, scaled[c][:, t * P : (t + 1) * P], t < 2 and c == 0, t != 1 and last)

        def weigh(t, tag):
            turned = psum.tile([P, S // P, P], F32, name=f"turned{t}", tag=tag)
            turn(turned, picked[t], S // P)
            weighted = keep.tile([P, S // P, P], F32, name=f"weighted{t}", align_bytes=64)
            for c in range(S // P):
                nc.scalar.activation(
                    weighted[:, c, :],
                    turned[:, c, :],
                    ACT.Identity,
                    scale=bow100[:, c : c + 1],
                    bias=shift[:, c : c + 1],
                )
            return weighted

        def add_weighted(t, closes_group):
            for c in range(S // P):
                add_turned(t, c, weighted[t][:, c, :], False, closes_group and c == S // P - 1)

        for t in (2, 3):
            for c in range(S // P):
                add_turned(t, c, shift[:, c : c + 1].to_broadcast([P, P]), c == 0, False)
        weighted = [weigh(0, "bank_z")]
        add_scaled(0)
        add_scaled(1)
        weighted.append(weigh(1, "bank_row"))
        add_scaled(2)
        add_weighted(0, False)
        add_scaled(3)
        add_weighted(1, True)
        for t in (0, 1):
            result = keep.tile([P, S], F32, name=f"result{t}", align_bytes=64)
            nc.scalar.copy(result[:], out_banks[t][:])
            nc.scalar.dma_start(out[t * P : (t + 1) * P, :], result[:])

        backoff = keep.tile([P, 2 * S], F32, name="backoff", tag="exp_y3", align_bytes=64)
        for t in (2, 3):
            nc.vector.tensor_tensor(
                backoff[:, (t - 2) * S : (t - 1) * S], plow_late[t - 2][:].indirect(suf_sb[:]), bow_row, ALU.mult
            )

        for t, pieces in ((2, 1), (3, 2)):
            result = keep.tile([P, S], F32, name=f"result{t}", align_bytes=64)
            width = S // pieces
            for first in range(0, S, width):
                cols = slice(first, first + width)
                term = backoff[:, (t - 2) * S + first : (t - 2) * S + first + width]
                nc.vector.tensor_tensor(result[:, cols], out_banks[t][:, cols], term, ALU.add)
                nc.sync.dma_start(out[t * P : (t + 1) * P, cols], result[:, cols])
